import numpy as np
import ml_dtypes


def mxq(x, axis, fmt="e4m3"):
    dtype, down = {"e4m3": (ml_dtypes.float8_e4m3fn, 7), "e5m2": (ml_dtypes.float8_e5m2, 14)}[fmt]
    v = np.moveaxis(np.asarray(x, np.float32).astype(ml_dtypes.bfloat16).astype(np.float64), axis, -1)
    blocks = v.reshape(v.shape[:-1] + (-1, 32))
    amax = np.abs(blocks).max(-1, keepdims=True)
    byte = np.maximum(np.where(amax > 0, np.frexp(amax)[1] - 1 + 127, 0) - down, 1)
    scale = np.exp2(byte - 127.0)
    codes = (blocks / scale).astype(np.float32).astype(dtype).astype(np.float64)
    return np.moveaxis((codes * scale).reshape(v.shape), -1, axis)


WIDE = False


def mx_kscale(k):
    if not WIDE:
        return np.ones(k)
    levels = np.array([10, -10, 5, -5, 0])
    if k % 512:
        return np.exp2(np.random.permutation(np.resize(levels, k // 32))).repeat(32)
    a = np.empty((k // 512, 16))
    for p in range(k // 512):
        a[p, :8] = np.random.permutation(np.resize(levels, 8))
        for g in range(8):
            far = levels[np.abs(levels - a[p, g]) >= 10]
            a[p, g + 8] = far[np.random.randint(len(far))]
    return np.exp2(a.ravel()).repeat(32)


def f64(x):
    return np.asarray(x).astype(np.float64)


def striped(idx):
    return np.tile(np.asarray(idx).reshape(-1, 16).T, (8, 1)).astype(np.uint16)


def unstriped(offs):
    return offs[:16].T.reshape(-1).astype(np.int64)


B, N, C, D, NQ = 1, 256, 4096, 512, 256


def eight(codes):
    return np.concatenate([codes[h].reshape(-1, 16).T for h in range(8)]).astype(np.uint16)


def uneight(offs):
    return np.stack([offs[16 * h:16 * h + 16].T.reshape(-1) for h in range(8)]).astype(np.int64)


def setup_inputs():
    n = np.random.standard_normal
    s = mx_kscale(D)[:, None]
    grid = lambda x: np.round(x * 32) / 32
    return {
        "qT": (n((B, D, NQ)) * s / np.sqrt(D)).astype(np.float32),
        "cb": (grid(n((D, C))) / s).astype(np.float32),
        "norm": np.tile(np.random.randint(32, 129, N) / 64.0, (128, 1)).astype(np.float32),
        "bias": np.tile(n(N), (128, 1)).astype(np.float32),
        "offs": eight(np.random.randint(0, C, (8, N))),
    }


def reference(qT, cb, norm, bias, offs):
    k = []
    for part, offs_ in enumerate((offs,)):
        codes = uneight(offs_)
        k += [f64(cb)[512 * part + 64 * h:512 * part + 64 * h + 64][:, codes[h]] for h in range(8)]
    k = np.concatenate(k) * f64(norm)[:1]
    a = mxq(f64(qT), 1, "e4m3").transpose(0, 2, 1) @ mxq(k, 0, "e4m3")
    a = a + f64(bias)[:1]
    return a

@@ -1,0 +1,96 @@
+import concourse.mybir as mybir
+
+F32 = mybir.dt.float32
+BF16 = mybir.dt.bfloat16
+U32 = mybir.dt.uint32
+U16 = mybir.dt.uint16
+U8 = mybir.dt.uint8
+FP8X4 = mybir.dt.float8_e4m3fn_x4
+MULT = mybir.AluOpType.mult
+ADD = mybir.AluOpType.add
+
+P = 128
+PACK = 4
+N = 256
+NQ = 256
+D = 512
+HALF = 128
+FLOPS = 2 * NQ * N * D
+
+
+def tile_attend_pq_lin_bias_kernel(tc, qT, cb, norm, bias, offs, out):
+    nc = tc.nc
+    with (
+        tc.tile_pool(name="keep", bufs=1) as keep,
+        tc.psum_pool(name="psum", bufs=1) as psum,
+    ):
+        planes = [keep.tile([P, 4096], F32, name=f"plane{t}") for t in range(PACK)]
+        lists = keep.tile([P, N // 16], U16, name="lists")
+        norm_sb = keep.tile([P, N], F32, name="norm_sb")
+        bias_sb = keep.tile([P, N], F32, name="bias_sb")
+        q_raw = keep.tile([P, PACK, NQ], F32, name="q_raw")
+
+        cb_rows = cb.rearrange("(p t) c -> p t c", t=PACK)
+        nc.sync.dma_start(planes[0][:], cb_rows[:, 0, :])
+        nc.sync.dma_start(lists[:], offs)
+        nc.sync.dma_start(norm_sb[:], norm)
+        nc.sync.dma_start(q_raw[:], qT[0, :, :].rearrange("(p t) q -> p t q", t=PACK))
+        for t in range(1, PACK):
+            nc.sync.dma_start(planes[t][:], cb_rows[:, t, :])
+        nc.sync.dma_start(bias_sb[:], bias)
+
+        q_grouped = keep.tile([P, NQ, PACK], BF16, name="q_grouped", align_bytes=64)
+        q_codes = keep.tile([P, NQ], U32, name="q_codes", align_bytes=64)
+        q_scales = keep.tile([P, NQ], U8, name="q_scales", align_bytes=64)
+        nc.scalar.copy(q_grouped[:], q_raw[:].rearrange("p t q -> p q t"))
+        nc.vector.quantize_mx(
+            out=q_codes[:].bitcast(FP8X4),
+            scales=q_scales[:],
+            in_=q_grouped[:].rearrange("p q t -> p (q t)"),
+        )
+
+        gathered = [keep.tile([P, PACK, HALF], F32, name=f"gathered{h}") for h in range(2)]
+        grouped = [keep.tile([P, HALF, PACK], BF16, name=f"grouped{h}", align_bytes=64) for h in range(2)]
+        codes = [keep.tile([P, HALF], U32, name=f"codes{h}", align_bytes=64) for h in range(2)]
+        scales = [keep.tile([P, HALF], U8, name=f"scales{h}", align_bytes=64) for h in range(2)]
+        acc = [psum.tile([P, 2, HALF], F32, name=f"acc{h}") for h in range(2)]
+        result = [keep.tile([P, 2, HALF], F32, name=f"result{h}") for h in range(2)]
+
+        for t in range(PACK):
+            for h in range(2):
+                nc.vector.tensor_tensor(
+                    gathered[h][:, t, :],
+                    planes[t][:].indirect(lists[:, 8 * h : 8 * h + 8]),
+                    norm_sb[:, HALF * h : HALF * h + HALF],
+                    MULT,
+                )
+            for h in range(2):
+                nc.vector.tensor_copy(grouped[h][:, :, t], gathered[h][:, t, :])
+        for h in range(2):
+            nc.vector.quantize_mx(
+                out=codes[h][:].bitcast(FP8X4),
+                scales=scales[h][:],
+                in_=grouped[h][:].rearrange("p n t -> p (n t)"),
+            )
+        out_rows = out[0, :, :].rearrange("(b p) n -> p b n", p=P)
+        for h in range(2):
+            for b in range(2):
+                q_cols = slice(P * b, P * b + P)
+                nc.tensor.matmul_mx(
+                    out=acc[h][:, b, :],
+                    lhsT=q_codes[:, q_cols].bitcast(FP8X4),
+                    lhsT_scale=q_scales[:, q_cols],
+                    rhs=codes[h][:].bitcast(FP8X4),
+                    rhs_scale=scales[h][:],
+                    start=True,
+                    stop=True,
+                )
+        for h in range(2):
+            n_cols = slice(HALF * h, HALF * h + HALF)
+            nc.vector.tensor_tensor(
+                result[h][:],
+                acc[h][:],
+                bias_sb[:, n_cols].unsqueeze(1).to_broadcast([P, 2, HALF]),
+                ADD,
+            )
+            nc.sync.dma_start(out_rows[:, :, n_cols], result[h][:])

@@ -1,4 +1,5 @@
 import concourse.mybir as mybir
+from concourse.masks import make_identity
 
 F32 = mybir.dt.float32
 BF16 = mybir.dt.bfloat16
@@ -30,14 +31,28 @@ def tile_attend_pq_lin_bias_kernel(tc, qT, cb, norm, bias, offs, out):
         bias_sb = keep.tile([P, N], F32, name="bias_sb")
         q_raw = keep.tile([P, PACK, NQ], F32, name="q_raw")
 
+        norm_rows = keep.tile([P, P], F32, name="norm_rows")
+        identity = keep.tile([P, P], F32, name="identity")
+        nc.gpsimd.memset(norm_rows[:], 0.0)
+        make_identity(nc, identity[:])
+
         cb_rows = cb.rearrange("(p t) c -> p t c", t=PACK)
         nc.sync.dma_start(planes[0][:], cb_rows[:, 0, :])
         nc.sync.dma_start(lists[:], offs)
-        nc.sync.dma_start(norm_sb[:], norm)
+        nc.sync.dma_start(norm_rows[0:2, :], norm[0:1, :].rearrange("o (u n) -> (o u) n", u=2))
         nc.sync.dma_start(q_raw[:], qT[0, :, :].rearrange("(p t) q -> p t q", t=PACK))
         for t in range(1, PACK):
             nc.sync.dma_start(planes[t][:], cb_rows[:, t, :])
         nc.sync.dma_start(bias_sb[:], bias)
+
+        norm_turned = psum.tile([P, P], F32, name="norm_turned")
+        norm_cols = keep.tile([P, 2], F32, name="norm_cols")
+        norm_spread = psum.tile([P, 2, P], F32, name="norm_spread")
+        nc.tensor.transpose(norm_turned[:], norm_rows[:], identity[:])
+        nc.scalar.copy(norm_cols[:], norm_turned[:, 0:2])
+        for u in range(2):
+            nc.tensor.transpose(norm_spread[:, u, :], norm_cols[:, u : u + 1].to_broadcast([P, P]), identity[:])
+        nc.scalar.copy(norm_sb[:], norm_spread[:].rearrange("p u n -> p (u n)"))
 
         q_grouped = keep.tile([P, NQ, PACK], BF16, name="q_grouped", align_bytes=64)
         q_codes = keep.tile([P, NQ], U32, name="q_codes", align_bytes=64)
@@ -53,8 +68,8 @@ def tile_attend_pq_lin_bias_kernel(tc, qT, cb, norm, bias, offs, out):
         grouped = [keep.tile([P, HALF, PACK], BF16, name=f"grouped{h}", align_bytes=64) for h in range(2)]
         codes = [keep.tile([P, HALF], U32, name=f"codes{h}", align_bytes=64) for h in range(2)]
         scales = [keep.tile([P, HALF], U8, name=f"scales{h}", align_bytes=64) for h in range(2)]
-        acc = [psum.tile([P, 2, HALF], F32, name=f"acc{h}") for h in range(2)]
-        result = [keep.tile([P, 2, HALF], F32, name=f"result{h}") for h in range(2)]
+        acc = [[psum.tile([P, HALF], F32, name=f"acc{h}{b}") for b in range(2)] for h in range(2)]
+        result = [[keep.tile([P, HALF], F32, name=f"result{h}{b}") for b in range(2)] for h in range(2)]
 
         for t in range(PACK):
             for h in range(2):
@@ -72,12 +87,11 @@ def tile_attend_pq_lin_bias_kernel(tc, qT, cb, norm, bias, offs, out):
                 scales=scales[h][:],
                 in_=grouped[h][:].rearrange("p n t -> p (n t)"),
             )
-        out_rows = out[0, :, :].rearrange("(b p) n -> p b n", p=P)
         for h in range(2):
             for b in range(2):
                 q_cols = slice(P * b, P * b + P)
                 nc.tensor.matmul_mx(
-                    out=acc[h][:, b, :],
+                    out=acc[h][b][:],
                     lhsT=q_codes[:, q_cols].bitcast(FP8X4),
                     lhsT_scale=q_scales[:, q_cols],
                     rhs=codes[h][:].bitcast(FP8X4),
@@ -87,10 +101,7 @@ def tile_attend_pq_lin_bias_kernel(tc, qT, cb, norm, bias, offs, out):
                 )
         for h in range(2):
             n_cols = slice(HALF * h, HALF * h + HALF)
-            nc.vector.tensor_tensor(
-                result[h][:],
-                acc[h][:],
-                bias_sb[:, n_cols].unsqueeze(1).to_broadcast([P, 2, HALF]),
-                ADD,
-            )
-            nc.sync.dma_start(out_rows[:, :, n_cols], result[h][:])
+            for b in range(2):
+                nc.vector.tensor_tensor(result[h][b][:], acc[h][b][:], bias_sb[:, n_cols], ADD)
+                store = nc.sync if b == 0 else nc.scalar
+                store.dma_start(out[0, P * b : P * b + P, n_cols], result[h][b][:])

import concourse.mybir as mybir
from concourse.masks import make_identity

F32 = mybir.dt.float32
BF16 = mybir.dt.bfloat16
U32 = mybir.dt.uint32
U16 = mybir.dt.uint16
U8 = mybir.dt.uint8
FP8X4 = mybir.dt.float8_e4m3fn_x4
MULT = mybir.AluOpType.mult
ADD = mybir.AluOpType.add

P = 128
PACK = 4
N = 256
NQ = 256
D = 512
HALF = 128
FLOPS = 2 * NQ * N * D


def tile_attend_pq_lin_bias_kernel(tc, qT, cb, norm, bias, offs, out):
    nc = tc.nc
    with (
        tc.tile_pool(name="keep", bufs=1) as keep,
        tc.psum_pool(name="psum", bufs=1) as psum,
    ):
        planes = [keep.tile([P, 4096], F32, name=f"plane{t}") for t in range(PACK)]
        lists = keep.tile([P, N // 16], U16, name="lists")
        norm_sb = keep.tile([P, N], F32, name="norm_sb")
        bias_sb = keep.tile([P, N], F32, name="bias_sb")
        q_raw = keep.tile([P, PACK, NQ], F32, name="q_raw")

        norm_rows = keep.tile([P, P], F32, name="norm_rows")
        identity = keep.tile([P, P], F32, name="identity")
        nc.gpsimd.memset(norm_rows[:], 0.0)
        make_identity(nc, identity[:])

        cb_rows = cb.rearrange("(p t) c -> p t c", t=PACK)
        nc.sync.dma_start(planes[0][:], cb_rows[:, 0, :])
        nc.sync.dma_start(lists[:], offs)
        nc.sync.dma_start(norm_rows[0:2, :], norm[0:1, :].rearrange("o (u n) -> (o u) n", u=2))
        nc.sync.dma_start(q_raw[:], qT[0, :, :].rearrange("(p t) q -> p t q", t=PACK))
        for t in range(1, PACK):
            nc.sync.dma_start(planes[t][:], cb_rows[:, t, :])
        nc.sync.dma_start(bias_sb[:], bias)

        norm_turned = psum.tile([P, P], F32, name="norm_turned")
        norm_cols = keep.tile([P, 2], F32, name="norm_cols")
        norm_spread = psum.tile([P, 2, P], F32, name="norm_spread")
        nc.tensor.transpose(norm_turned[:], norm_rows[:], identity[:])
        nc.scalar.copy(norm_cols[:], norm_turned[:, 0:2])
        for u in range(2):
            nc.tensor.transpose(norm_spread[:, u, :], norm_cols[:, u : u + 1].to_broadcast([P, P]), identity[:])
        nc.scalar.copy(norm_sb[:], norm_spread[:].rearrange("p u n -> p (u n)"))

        q_grouped = keep.tile([P, NQ, PACK], BF16, name="q_grouped", align_bytes=64)
        q_codes = keep.tile([P, NQ], U32, name="q_codes", align_bytes=64)
        q_scales = keep.tile([P, NQ], U8, name="q_scales", align_bytes=64)
        nc.scalar.copy(q_grouped[:], q_raw[:].rearrange("p t q -> p q t"))
        nc.vector.quantize_mx(
            out=q_codes[:].bitcast(FP8X4),
            scales=q_scales[:],
            in_=q_grouped[:].rearrange("p q t -> p (q t)"),
        )

        gathered = [keep.tile([P, PACK, HALF], F32, name=f"gathered{h}") for h in range(2)]
        grouped = [keep.tile([P, HALF, PACK], BF16, name=f"grouped{h}", align_bytes=64) for h in range(2)]
        codes = [keep.tile([P, HALF], U32, name=f"codes{h}", align_bytes=64) for h in range(2)]
        scales = [keep.tile([P, HALF], U8, name=f"scales{h}", align_bytes=64) for h in range(2)]
        acc = [[psum.tile([P, HALF], F32, name=f"acc{h}{b}") for b in range(2)] for h in range(2)]
        result = [[keep.tile([P, HALF], F32, name=f"result{h}{b}") for b in range(2)] for h in range(2)]

        for t in range(PACK):
            for h in range(2):
                nc.vector.tensor_tensor(
                    gathered[h][:, t, :],
                    planes[t][:].indirect(lists[:, 8 * h : 8 * h + 8]),
                    norm_sb[:, HALF * h : HALF * h + HALF],
                    MULT,
                )
            for h in range(2):
                nc.vector.tensor_copy(grouped[h][:, :, t], gathered[h][:, t, :])
        for h in range(2):
            nc.vector.quantize_mx(
                out=codes[h][:].bitcast(FP8X4),
                scales=scales[h][:],
                in_=grouped[h][:].rearrange("p n t -> p (n t)"),
            )
        for h in range(2):
            for b in range(2):
                q_cols = slice(P * b, P * b + P)
                nc.tensor.matmul_mx(
                    out=acc[h][b][:],
                    lhsT=q_codes[:, q_cols].bitcast(FP8X4),
                    lhsT_scale=q_scales[:, q_cols],
                    rhs=codes[h][:].bitcast(FP8X4),
                    rhs_scale=scales[h][:],
                    start=True,
                    stop=True,
                )
        for h in range(2):
            n_cols = slice(HALF * h, HALF * h + HALF)
            for b in range(2):
                nc.vector.tensor_tensor(result[h][b][:], acc[h][b][:], bias_sb[:, n_cols], ADD)
                store = nc.sync if b == 0 else nc.scalar
                store.dma_start(out[0, P * b : P * b + P, n_cols], result[h][b][:])
